import numpy as np
import ml_dtypes


def mxq(x, axis, fmt="e4m3"):
    dtype, down = {"e4m3": (ml_dtypes.float8_e4m3fn, 7), "e5m2": (ml_dtypes.float8_e5m2, 14)}[fmt]
    v = np.moveaxis(np.asarray(x, np.float32).astype(ml_dtypes.bfloat16).astype(np.float64), axis, -1)
    blocks = v.reshape(v.shape[:-1] + (-1, 32))
    amax = np.abs(blocks).max(-1, keepdims=True)
    byte = np.maximum(np.where(amax > 0, np.frexp(amax)[1] - 1 + 127, 0) - down, 1)
    scale = np.exp2(byte - 127.0)
    codes = (blocks / scale).astype(np.float32).astype(dtype).astype(np.float64)
    return np.moveaxis((codes * scale).reshape(v.shape), -1, axis)


WIDE = False


def mx_kscale(k, group=512):
    if not WIDE:
        return np.ones(k)
    levels = np.array([18, -18])
    if group != 512:
        return np.exp2(np.random.permutation(np.resize(levels, k // group))).repeat(group)
    if k % 512:
        return np.exp2(np.random.permutation(np.resize(levels, k // 32))).repeat(32)
    a = np.empty((k // 512, 16))
    for p in range(k // 512):
        a[p, :8] = np.random.permutation(np.resize(levels, 8))
        for g in range(8):
            far = levels[np.abs(levels - a[p, g]) >= 10]
            a[p, g + 8] = far[np.random.randint(len(far))]
    return np.exp2(a.ravel()).repeat(32)


def f64(x):
    return np.asarray(x).astype(np.float64)


G, D, M, N, K = 4, 128, 128, 512, 128


def sgn(shape):
    return np.random.uniform(0.5, 2.0, shape) * np.where(np.random.standard_normal(shape) < 0, -1.0, 1.0)


def setup_inputs():
    n = np.random.standard_normal
    s_d = mx_kscale(D, 0)
    s_m = mx_kscale(M, 0)
    return {
        "h": (n((G, D, N)) * s_d[:, None]).astype(np.float32),
        "w1": (n((G, D, M)) / np.sqrt(D) / s_d[:, None]).astype(np.float32),
        "x1": (n((G, M, N))).astype(np.float32),
        "a1": (sgn((G, M, 1)) * s_m[:, None]).astype(np.float32),
        "w2": (n((G, M, K)) / np.sqrt(M) / s_m[:, None]).astype(np.float32),
        "x2": (n((G, K, N))).astype(np.float32),
    }


def reference(h, w1, x1, a1, w2, x2):
    w1q = mxq(f64(w1), 1, "e4m3")
    hq = mxq(f64(h), 1, "e4m3")
    z1 = w1q.transpose(0, 2, 1) @ hq
    h1 = np.tanh(z1 + f64(x1)) * f64(a1)
    w2q = mxq(f64(w2), 1, "e4m3")
    h1q = mxq(h1, 1, "e4m3")
    z2 = w2q.transpose(0, 2, 1) @ h1q
    y = np.tanh(z2 + f64(x2))
    return y

@@ -1,0 +1,141 @@
+from contextlib import ExitStack
+
+import concourse.mybir as mybir
+
+G, D, N = 4, 128, 512
+FLOPS = 2 * 2 * G * D * D * N
+
+F32 = mybir.dt.float32
+BF16 = mybir.dt.bfloat16
+U32 = mybir.dt.uint32
+U8 = mybir.dt.uint8
+FP8X4 = mybir.dt.float8_e4m3fn_x4
+ACT = mybir.ActivationFunctionType
+ALU = mybir.AluOpType
+
+P = 128
+PACK = 4
+ROWS = D // PACK
+HALVES = 2
+C = N // HALVES
+MM_N = 128
+RUN = 4
+SCALAR_COLS = 96
+
+
+def tile_rows_steps_tanh_kernel(tc, h, w1, x1, a1, w2, x2, out):
+    nc = tc.nc
+
+    with ExitStack() as ctx:
+        sb = ctx.enter_context(tc.tile_pool(name="sb", bufs=1))
+        ps = ctx.enter_context(tc.psum_pool(name="ps", bufs=1))
+        ctx.enter_context(tc.manual_schedule())
+
+        def tile(name, shape, dtype):
+            return sb.tile(shape, dtype, name=name, align_bytes=64)
+
+        def columns(half):
+            return slice(half * C, (half + 1) * C)
+
+        def interleave(copy, dst, src, lo, hi):
+            copy(
+                out=dst[:, lo:hi, :].rearrange("p (c i) j -> p c j i", i=RUN),
+                in_=src[:, :, lo:hi].rearrange("p j (c i) -> p c j i", i=RUN),
+            )
+
+        def quantize(name, grouped, width):
+            codes = tile(name + "_codes", [P, width], U32)
+            scales = tile(name + "_scales", [P, width], U8)
+            nc.vector.quantize_mx(
+                out=codes[:].bitcast(FP8X4), scales=scales[:], in_=grouped[:].rearrange("p c j -> p (c j)")
+            )
+            return codes, scales
+
+        banks = [[ps.tile([P, N], F32, name="bank_%d_%d" % (half, g)) for g in range(G)] for half in range(HALVES)]
+
+        def products(half, weights, state):
+            for g in range(G):
+                rows = slice(g * ROWS, (g + 1) * ROWS)
+                for n0 in range(0, C, MM_N):
+                    cols = slice(n0, n0 + MM_N)
+                    nc.tensor.matmul_mx(
+                        out=banks[half][g][:, cols],
+                        lhsT=weights[0][rows, :].bitcast(FP8X4),
+                        lhsT_scale=weights[1][rows, :],
+                        rhs=state[0][rows, cols].bitcast(FP8X4),
+                        rhs_scale=state[1][rows, cols],
+                        start=True,
+                        stop=True,
+                    )
+
+        h_rows = h.rearrange("g (p j) n -> (g p) j n", j=PACK)
+        x1_rows = x1.rearrange("g m n -> m g n")
+        x2_rows = x2.rearrange("g k n -> k g n")
+        out_rows = out.rearrange("g k n -> k g n")
+
+        a_rows = tile("a_rows", [P, P], F32)
+        nc.gpsimd.memset(a_rows[:], 0.0)
+        nc.scalar.dma_start(
+            out=a_rows[0:P:32, :].rearrange("q (g i) -> q g i", g=G),
+            in_=a1.rearrange("g (q i) o -> q g (i o)", i=32),
+        )
+
+        w1_raw = tile("w1_raw", [P, PACK, D], F32)
+        nc.sync.dma_start(out=w1_raw[:], in_=w1.rearrange("g (p j) m -> (g p) j m", j=PACK))
+        h_raw, x1_sb = [], []
+        for half in range(HALVES):
+            h_raw.append(tile("h_raw%d" % half, [P, PACK, C], F32))
+            nc.sync.dma_start(out=h_raw[half][:], in_=h_rows[:, :, columns(half)])
+            x1_sb.append(tile("x1_sb%d" % half, [P, G, C], F32))
+            nc.sync.dma_start(out=x1_sb[half][:], in_=x1_rows[:, :, columns(half)])
+        w2_raw = tile("w2_raw", [P, PACK, D], F32)
+        nc.sync.dma_start(out=w2_raw[:], in_=w2.rearrange("g (p j) k -> (g p) j k", j=PACK))
+
+        def prepare_weights(name, raw):
+            grouped = tile(name + "_grouped", [P, D, PACK], BF16)
+            interleave(nc.vector.tensor_copy, grouped, raw, 0, D)
+            return quantize(name, grouped, D)
+
+        def prepare_state(name, raw, scalar_cols):
+            grouped = tile(name + "_grouped", [P, C, PACK], BF16)
+            if scalar_cols:
+                interleave(nc.scalar.copy, grouped, raw, C - scalar_cols, C)
+            interleave(nc.vector.tensor_copy, grouped, raw, 0, C - scalar_cols)
+            return quantize(name, grouped, C)
+
+        def step1(half):
+            moved = tile("moved%d" % half, [P, PACK, C], BF16)
+            for g in range(G):
+                pre = tile("pre1_%d_%d" % (half, g), [P, C], F32)
+                nc.vector.tensor_tensor(out=pre[:], in0=banks[half][g][:, 0:C], in1=x1_sb[half][:, g, :], op=ALU.add)
+                act = tile("act1_%d_%d" % (half, g), [P, C], F32)
+                nc.scalar.activation(out=act[:], in_=pre[:], func=ACT.Tanh)
+                h1 = tile("h1_%d_%d" % (half, g), [P, C], BF16)
+                nc.gpsimd.tensor_scalar(
+                    out=h1[:], in0=act[:], scalar1=a_cols[:, 32 * g : 32 * g + 1], scalar2=0.0, op0=ALU.mult, op1=ALU.add
+                )
+                nc.sync.dma_start(out=moved[g * ROWS : (g + 1) * ROWS, :, :], in_=h1[:])
+            return moved
+
+        def step2(half):
+            for g in range(G):
+                pre = tile("pre2_%d_%d" % (half, g), [P, C], F32)
+                nc.vector.tensor_tensor(out=pre[:], in0=banks[half][g][:, 0:C], in1=x2_sb[:, g, columns(half)], op=ALU.add)
+                y = tile("y_%d_%d" % (half, g), [P, C], F32)
+                nc.scalar.activation(out=y[:], in_=pre[:], func=ACT.Tanh)
+                nc.sync.dma_start(out=out_rows[:, g, columns(half)], in_=y[:])
+
+        w1q = prepare_weights("w1", w1_raw)
+        a_cols = tile("a_cols", [P, P], F32)
+        nc.vector.transpose(out=a_cols[:], in_=a_rows[:])
+        products(0, w1q, prepare_state("h0", h_raw[0], SCALAR_COLS))
+        moved0 = step1(0)
+        x2_sb = tile("x2_sb", [P, G, N], F32)
+        nc.sync.dma_start(out=x2_sb[:], in_=x2_rows)
+        products(1, w1q, prepare_state("h1", h_raw[1], 0))
+        w2q = prepare_weights("w2", w2_raw)
+        moved1 = step1(1)
+        products(0, w2q, prepare_state("s0", moved0, 0))
+        step2(0)
+        products(1, w2q, prepare_state("s1", moved1, SCALAR_COLS))
+        step2(1)

@@ -21,6 +21,7 @@ C = N // HALVES
 MM_N = 128
 RUN = 4
 SCALAR_COLS = 96
+SCALAR_MULS = (0,)
 
 
 def tile_rows_steps_tanh_kernel(tc, h, w1, x1, a1, w2, x2, out):
@@ -82,60 +83,88 @@ def tile_rows_steps_tanh_kernel(tc, h, w1, x1, a1, w2, x2, out):
 
         w1_raw = tile("w1_raw", [P, PACK, D], F32)
         nc.sync.dma_start(out=w1_raw[:], in_=w1.rearrange("g (p j) m -> (g p) j m", j=PACK))
-        h_raw, x1_sb = [], []
+        h_raw = []
         for half in range(HALVES):
             h_raw.append(tile("h_raw%d" % half, [P, PACK, C], F32))
             nc.sync.dma_start(out=h_raw[half][:], in_=h_rows[:, :, columns(half)])
-            x1_sb.append(tile("x1_sb%d" % half, [P, G, C], F32))
-            nc.sync.dma_start(out=x1_sb[half][:], in_=x1_rows[:, :, columns(half)])
+        x1_sb = {}
+        for half in range(HALVES):
+            for pair in range(2):
+                t = tile("x1_sb%d_%d" % (half, pair), [P, 2, C], F32)
+                nc.sync.dma_start(out=t[:], in_=x1_rows[:, 2 * pair : 2 * pair + 2, columns(half)])
+                x1_sb[half, 2 * pair], x1_sb[half, 2 * pair + 1] = t[:, 0, :], t[:, 1, :]
         w2_raw = tile("w2_raw", [P, PACK, D], F32)
         nc.sync.dma_start(out=w2_raw[:], in_=w2.rearrange("g (p j) k -> (g p) j k", j=PACK))
+        x2_sb = {}
 
-        def prepare_weights(name, raw):
-            grouped = tile(name + "_grouped", [P, D, PACK], BF16)
-            interleave(nc.vector.tensor_copy, grouped, raw, 0, D)
-            return quantize(name, grouped, D)
+        def load_x2(pair):
+            t = tile("x2_sb%d" % pair, [P, 2, N], F32)
+            nc.sync.dma_start(out=t[:], in_=x2_rows[:, 2 * pair : 2 * pair + 2, :])
+            x2_sb[2 * pair], x2_sb[2 * pair + 1] = t[:, 0, :], t[:, 1, :]
 
-        def prepare_state(name, raw, scalar_cols):
-            grouped = tile(name + "_grouped", [P, C, PACK], BF16)
+        def group(name, raw, width, scalar_cols):
+            grouped = tile(name + "_grouped", [P, width, PACK], BF16)
             if scalar_cols:
-                interleave(nc.scalar.copy, grouped, raw, C - scalar_cols, C)
-            interleave(nc.vector.tensor_copy, grouped, raw, 0, C - scalar_cols)
-            return quantize(name, grouped, C)
+                interleave(nc.scalar.copy, grouped, raw, width - scalar_cols, width)
+            interleave(nc.vector.tensor_copy, grouped, raw, 0, width - scalar_cols)
+            return grouped
 
-        def step1(half):
-            moved = tile("moved%d" % half, [P, PACK, C], BF16)
-            for g in range(G):
-                pre = tile("pre1_%d_%d" % (half, g), [P, C], F32)
-                nc.vector.tensor_tensor(out=pre[:], in0=banks[half][g][:, 0:C], in1=x1_sb[half][:, g, :], op=ALU.add)
-                act = tile("act1_%d_%d" % (half, g), [P, C], F32)
-                nc.scalar.activation(out=act[:], in_=pre[:], func=ACT.Tanh)
-                h1 = tile("h1_%d_%d" % (half, g), [P, C], BF16)
-                nc.gpsimd.tensor_scalar(
-                    out=h1[:], in0=act[:], scalar1=a_cols[:, 32 * g : 32 * g + 1], scalar2=0.0, op0=ALU.mult, op1=ALU.add
-                )
-                nc.sync.dma_start(out=moved[g * ROWS : (g + 1) * ROWS, :, :], in_=h1[:])
-            return moved
+        moved = [tile("moved%d" % half, [P, PACK, C], BF16) for half in range(HALVES)]
+        act1 = {}
 
-        def step2(half):
-            for g in range(G):
-                pre = tile("pre2_%d_%d" % (half, g), [P, C], F32)
-                nc.vector.tensor_tensor(out=pre[:], in0=banks[half][g][:, 0:C], in1=x2_sb[:, g, columns(half)], op=ALU.add)
-                y = tile("y_%d_%d" % (half, g), [P, C], F32)
+        def add_tanh1(half, g):
+            pre = tile("pre1_%d_%d" % (half, g), [P, C], F32)
+            nc.vector.tensor_tensor(out=pre[:], in0=banks[half][g][:, 0:C], in1=x1_sb[half, g], op=ALU.add)
+            act1[half, g] = tile("act1_%d_%d" % (half, g), [P, C], F32)
+            nc.scalar.activation(out=act1[half, g][:], in_=pre[:], func=ACT.Tanh)
+
+        def scale_move(half, g):
+            h1 = tile("h1_%d_%d" % (half, g), [P, C], BF16)
+            a_col = a_cols[:, 32 * g : 32 * g + 1]
+            if g in SCALAR_MULS:
+                nc.scalar.activation(out=h1[:], in_=act1[half, g][:], func=ACT.Copy, scale=a_col)
+            else:
+                nc.vector.tensor_scalar(out=h1[:], in0=act1[half, g][:], scalar1=a_col, scalar2=None, op0=ALU.mult)
+            nc.sync.dma_start(out=moved[half][g * ROWS : (g + 1) * ROWS, :, :], in_=h1[:])
+            if g == G - 1:
+                load_x2(half)
+
+        y0 = tile("y0", [P, G, C], F32)
+
+        def step2(half, g):
+            pre = tile("pre2_%d_%d" % (half, g), [P, C], F32)
+            nc.vector.tensor_tensor(out=pre[:], in0=banks[half][g][:, 0:C], in1=x2_sb[g][:, columns(half)], op=ALU.add)
+            if half == 0:
+                nc.scalar.activation(out=y0[:, g, :], in_=pre[:], func=ACT.Tanh)
+                if g % 2 == 1:
+                    nc.sync.dma_start(out=out_rows[:, g - 1 : g + 1, columns(half)], in_=y0[:, g - 1 : g + 1, :])
+            else:
+                y = tile("y_%d" % g, [P, C], F32)
                 nc.scalar.activation(out=y[:], in_=pre[:], func=ACT.Tanh)
                 nc.sync.dma_start(out=out_rows[:, g, columns(half)], in_=y[:])
 
-        w1q = prepare_weights("w1", w1_raw)
+        w1q = quantize("w1", group("w1", w1_raw, D, 0), D)
         a_cols = tile("a_cols", [P, P], F32)
-        nc.vector.transpose(out=a_cols[:], in_=a_rows[:])
-        products(0, w1q, prepare_state("h0", h_raw[0], SCALAR_COLS))
-        moved0 = step1(0)
-        x2_sb = tile("x2_sb", [P, G, N], F32)
-        nc.sync.dma_start(out=x2_sb[:], in_=x2_rows)
-        products(1, w1q, prepare_state("h1", h_raw[1], 0))
-        w2q = prepare_weights("w2", w2_raw)
-        moved1 = step1(1)
-        products(0, w2q, prepare_state("s0", moved0, 0))
-        step2(0)
-        products(1, w2q, prepare_state("s1", moved1, SCALAR_COLS))
-        step2(1)
+        for half in range(HALVES):
+            grouped = group("h%d" % half, h_raw[half], C, SCALAR_COLS)
+            if half == 0:
+                nc.vector.transpose(out=a_cols[:], in_=a_rows[:])
+            products(half, w1q, quantize("h%d" % half, grouped, C))
+        units = [(half, g) for half in range(HALVES) for g in range(G)]
+        for i, unit in enumerate(units):
+            add_tanh1(*unit)
+            if i >= 1:
+                scale_move(*units[i - 1])
+        w2_grouped = group("w2", w2_raw, D, 0)
+        scale_move(*units[-1])
+        s0_grouped = group("s0", moved[0], C, SCALAR_COLS)
+        w2q = quantize("w2", w2_grouped, D)
+        products(0, w2q, quantize("s0", s0_grouped, C))
+        step2(0, 0)
+        step2(0, 1)
+        s1_grouped = group("s1", moved[1], C, SCALAR_COLS)
+        step2(0, 2)
+        products(1, w2q, quantize("s1", s1_grouped, C))
+        step2(0, 3)
+        for g in range(G):
+            step2(1, g)

@@ -20,8 +20,9 @@ HALVES = 2
 C = N // HALVES
 MM_N = 128
 RUN = 4
+SQUARE = 32
+SCALAR_COLS_FIRST = 64
 SCALAR_COLS = 96
-SCALAR_MULS = (0,)
 
 
 def tile_rows_steps_tanh_kernel(tc, h, w1, x1, a1, w2, x2, out):
@@ -38,13 +39,49 @@ def tile_rows_steps_tanh_kernel(tc, h, w1, x1, a1, w2, x2, out):
         def columns(half):
             return slice(half * C, (half + 1) * C)
 
-        def interleave(copy, dst, src, lo, hi):
-            copy(
-                out=dst[:, lo:hi, :].rearrange("p (c i) j -> p c j i", i=RUN),
-                in_=src[:, :, lo:hi].rearrange("p j (c i) -> p c j i", i=RUN),
-            )
+        banks = [[ps.tile([P, N], F32, name="bank_%d_%d" % (half, g)) for g in range(G)] for half in range(HALVES)]
 
-        def quantize(name, grouped, width):
+        def load_operand(name, src, cols):
+            raw = tile(name, [P, PACK, cols.stop - cols.start], F32)
+            nc.sync.dma_start(out=raw[:], in_=src.rearrange("g (p j) c -> (g p) j c", j=PACK)[:, :, cols])
+            return raw[:]
+
+        def load_addend(name, src, heads, cols):
+            sbuf = tile(name, [P, len(heads), cols.stop - cols.start], F32)
+            nc.sync.dma_start(out=sbuf[:], in_=src.rearrange("g m n -> m g n")[:, heads.start : heads.stop, cols])
+            return [sbuf[:, g - heads.start, :] for g in heads]
+
+        a_rows = tile("a_rows", [P, G * SQUARE], F32)
+        nc.vector.memset(a_rows[:], 0.0)
+        nc.scalar.dma_start(
+            out=a_rows[0:P:SQUARE, :].rearrange("q (g i) -> q g i", g=G),
+            in_=a1.rearrange("g (q i) o -> q g (i o)", i=SQUARE),
+        )
+
+        w1_raw = load_operand("w1_raw", w1, slice(0, D))
+        h_raw = [load_operand("h_raw%d" % half, h, columns(half)) for half in range(HALVES)]
+        x1_sb = [[] for half in range(HALVES)]
+        for half in range(HALVES):
+            for g0 in range(0, G, 2):
+                x1_sb[half].extend(load_addend("x1_%d_%d" % (half, g0), x1, range(g0, g0 + 2), columns(half)))
+        w2_raw = load_operand("w2_raw", w2, slice(0, D))
+
+        x2_sb = load_addend("x2_0", x2, range(0, 1), slice(0, N))
+
+        def interleave(name, raw, scalar_cols):
+            width = raw.shape[2]
+            grouped = tile(name, [P, width, PACK], BF16)
+            split = width - scalar_cols
+            for copy, lo, hi in ((nc.scalar.copy, split, width), (nc.vector.tensor_copy, 0, split)):
+                if lo < hi:
+                    copy(
+                        out=grouped[:, lo:hi, :].rearrange("p (c i) j -> p c j i", i=RUN),
+                        in_=raw[:, :, lo:hi].rearrange("p j (c i) -> p c j i", i=RUN),
+                    )
+            return grouped
+
+        def quantize(name, grouped):
+            width = grouped[:].shape[1]
             codes = tile(name + "_codes", [P, width], U32)
             scales = tile(name + "_scales", [P, width], U8)
             nc.vector.quantize_mx(
@@ -52,119 +89,74 @@ def tile_rows_steps_tanh_kernel(tc, h, w1, x1, a1, w2, x2, out):
             )
             return codes, scales
 
-        banks = [[ps.tile([P, N], F32, name="bank_%d_%d" % (half, g)) for g in range(G)] for half in range(HALVES)]
-
         def products(half, weights, state):
+            (w_codes, w_scales), (s_codes, s_scales) = weights, state
             for g in range(G):
                 rows = slice(g * ROWS, (g + 1) * ROWS)
-                for n0 in range(0, C, MM_N):
-                    cols = slice(n0, n0 + MM_N)
+                for c0 in range(0, C, MM_N):
+                    cols = slice(c0, c0 + MM_N)
                     nc.tensor.matmul_mx(
                         out=banks[half][g][:, cols],
-                        lhsT=weights[0][rows, :].bitcast(FP8X4),
-                        lhsT_scale=weights[1][rows, :],
-                        rhs=state[0][rows, cols].bitcast(FP8X4),
-                        rhs_scale=state[1][rows, cols],
+                        lhsT=w_codes[rows, :].bitcast(FP8X4),
+                        lhsT_scale=w_scales[rows, :],
+                        rhs=s_codes[rows, cols].bitcast(FP8X4),
+                        rhs_scale=s_scales[rows, cols],
                         start=True,
                         stop=True,
                     )
 
-        h_rows = h.rearrange("g (p j) n -> (g p) j n", j=PACK)
-        x1_rows = x1.rearrange("g m n -> m g n")
-        x2_rows = x2.rearrange("g k n -> k g n")
-        out_rows = out.rearrange("g k n -> k g n")
+        def add_tanh(name, half, g, addend):
+            pre = tile(name + "_pre", [P, C], F32)
+            nc.vector.tensor_tensor(out=pre[:], in0=banks[half][g][:, 0:C], in1=addend, op=ALU.add)
+            act = tile(name + "_act", [P, C], F32)
+            nc.scalar.activation(out=act[:], in_=pre[:], func=ACT.Tanh)
+            return act
 
-        a_rows = tile("a_rows", [P, P], F32)
-        nc.gpsimd.memset(a_rows[:], 0.0)
-        nc.scalar.dma_start(
-            out=a_rows[0:P:32, :].rearrange("q (g i) -> q g i", g=G),
-            in_=a1.rearrange("g (q i) o -> q g (i o)", i=32),
-        )
+        a_cols = tile("a_cols", [P, G * SQUARE], F32)
+        folded = [tile("folded%d" % half, [P, PACK, C], BF16) for half in range(HALVES)]
+        tanh1 = {}
 
-        w1_raw = tile("w1_raw", [P, PACK, D], F32)
-        nc.sync.dma_start(out=w1_raw[:], in_=w1.rearrange("g (p j) m -> (g p) j m", j=PACK))
-        h_raw = []
-        for half in range(HALVES):
-            h_raw.append(tile("h_raw%d" % half, [P, PACK, C], F32))
-            nc.sync.dma_start(out=h_raw[half][:], in_=h_rows[:, :, columns(half)])
-        x1_sb = {}
-        for half in range(HALVES):
-            for pair in range(2):
-                t = tile("x1_sb%d_%d" % (half, pair), [P, 2, C], F32)
-                nc.sync.dma_start(out=t[:], in_=x1_rows[:, 2 * pair : 2 * pair + 2, columns(half)])
-                x1_sb[half, 2 * pair], x1_sb[half, 2 * pair + 1] = t[:, 0, :], t[:, 1, :]
-        w2_raw = tile("w2_raw", [P, PACK, D], F32)
-        nc.sync.dma_start(out=w2_raw[:], in_=w2.rearrange("g (p j) k -> (g p) j k", j=PACK))
-        x2_sb = {}
+        def step1(half, g):
+            tanh1[half, g] = add_tanh("step1_%d_%d" % (half, g), half, g, x1_sb[half][g])
 
-        def load_x2(pair):
-            t = tile("x2_sb%d" % pair, [P, 2, N], F32)
-            nc.sync.dma_start(out=t[:], in_=x2_rows[:, 2 * pair : 2 * pair + 2, :])
-            x2_sb[2 * pair], x2_sb[2 * pair + 1] = t[:, 0, :], t[:, 1, :]
-
-        def group(name, raw, width, scalar_cols):
-            grouped = tile(name + "_grouped", [P, width, PACK], BF16)
-            if scalar_cols:
-                interleave(nc.scalar.copy, grouped, raw, width - scalar_cols, width)
-            interleave(nc.vector.tensor_copy, grouped, raw, 0, width - scalar_cols)
-            return grouped
-
-        moved = [tile("moved%d" % half, [P, PACK, C], BF16) for half in range(HALVES)]
-        act1 = {}
-
-        def add_tanh1(half, g):
-            pre = tile("pre1_%d_%d" % (half, g), [P, C], F32)
-            nc.vector.tensor_tensor(out=pre[:], in0=banks[half][g][:, 0:C], in1=x1_sb[half, g], op=ALU.add)
-            act1[half, g] = tile("act1_%d_%d" % (half, g), [P, C], F32)
-            nc.scalar.activation(out=act1[half, g][:], in_=pre[:], func=ACT.Tanh)
-
-        def scale_move(half, g):
+        def scale_fold(half, g):
             h1 = tile("h1_%d_%d" % (half, g), [P, C], BF16)
-            a_col = a_cols[:, 32 * g : 32 * g + 1]
-            if g in SCALAR_MULS:
-                nc.scalar.activation(out=h1[:], in_=act1[half, g][:], func=ACT.Copy, scale=a_col)
-            else:
-                nc.vector.tensor_scalar(out=h1[:], in0=act1[half, g][:], scalar1=a_col, scalar2=None, op0=ALU.mult)
-            nc.sync.dma_start(out=moved[half][g * ROWS : (g + 1) * ROWS, :, :], in_=h1[:])
-            if g == G - 1:
-                load_x2(half)
-
-        y0 = tile("y0", [P, G, C], F32)
+            a_col = a_cols[:, SQUARE * g : SQUARE * g + 1]
+            nc.vector.tensor_scalar(out=h1[:], in0=tanh1[half, g][:], scalar1=a_col, scalar2=None, op0=ALU.mult)
+            nc.sync.dma_start(out=folded[half][g * ROWS : (g + 1) * ROWS, :, :], in_=h1[:])
 
         def step2(half, g):
-            pre = tile("pre2_%d_%d" % (half, g), [P, C], F32)
-            nc.vector.tensor_tensor(out=pre[:], in0=banks[half][g][:, 0:C], in1=x2_sb[g][:, columns(half)], op=ALU.add)
-            if half == 0:
-                nc.scalar.activation(out=y0[:, g, :], in_=pre[:], func=ACT.Tanh)
-                if g % 2 == 1:
-                    nc.sync.dma_start(out=out_rows[:, g - 1 : g + 1, columns(half)], in_=y0[:, g - 1 : g + 1, :])
-            else:
-                y = tile("y_%d" % g, [P, C], F32)
-                nc.scalar.activation(out=y[:], in_=pre[:], func=ACT.Tanh)
-                nc.sync.dma_start(out=out_rows[:, g, columns(half)], in_=y[:])
+            y = add_tanh("step2_%d_%d" % (half, g), half, g, x2_sb[g][:, columns(half)])
+            nc.sync.dma_start(out=out[g, :, columns(half)], in_=y[:])
 
-        w1q = quantize("w1", group("w1", w1_raw, D, 0), D)
-        a_cols = tile("a_cols", [P, P], F32)
-        for half in range(HALVES):
-            grouped = group("h%d" % half, h_raw[half], C, SCALAR_COLS)
-            if half == 0:
-                nc.vector.transpose(out=a_cols[:], in_=a_rows[:])
-            products(half, w1q, quantize("h%d" % half, grouped, C))
-        units = [(half, g) for half in range(HALVES) for g in range(G)]
-        for i, unit in enumerate(units):
-            add_tanh1(*unit)
-            if i >= 1:
-                scale_move(*units[i - 1])
-        w2_grouped = group("w2", w2_raw, D, 0)
-        scale_move(*units[-1])
-        s0_grouped = group("s0", moved[0], C, SCALAR_COLS)
-        w2q = quantize("w2", w2_grouped, D)
-        products(0, w2q, quantize("s0", s0_grouped, C))
+        w1_q = quantize("w1", interleave("w1_grouped", w1_raw, 0))
+        products(0, w1_q, quantize("h_early", interleave("h_early_grouped", h_raw[0], SCALAR_COLS_FIRST)))
+        h_late = interleave("h_late_grouped", h_raw[1], SCALAR_COLS)
+        nc.vector.transpose(out=a_cols[:], in_=a_rows[:])
+        step1(0, 0)
+        products(1, w1_q, quantize("h_late", h_late))
+        for g in range(1, G):
+            step1(0, g)
+        scale_fold(0, 0)
+        scale_fold(0, 1)
+        step1(1, 0)
+        scale_fold(0, 2)
+        scale_fold(0, 3)
+        x2_sb.extend(load_addend("x2_1", x2, range(1, 2), slice(0, N)))
+        for g in range(1, G):
+            step1(1, g)
+        for g in range(G):
+            scale_fold(1, g)
+        x2_sb.extend(load_addend("x2_2", x2, range(2, G), slice(0, N)))
+
+        w2_grouped = interleave("w2_grouped", w2_raw, D)
+        state0 = interleave("state0_grouped", folded[0][:], SCALAR_COLS)
+        w2_q = quantize("w2", w2_grouped)
+        products(0, w2_q, quantize("state0", state0))
+        state1 = interleave("state1_grouped", folded[1][:], SCALAR_COLS)
         step2(0, 0)
-        step2(0, 1)
-        s1_grouped = group("s1", moved[1], C, SCALAR_COLS)
-        step2(0, 2)
-        products(1, w2q, quantize("s1", s1_grouped, C))
-        step2(0, 3)
+        products(1, w2_q, quantize("state1", state1))
+        for g in range(1, G):
+            step2(0, g)
         for g in range(G):
             step2(1, g)

from contextlib import ExitStack

import concourse.mybir as mybir

G, D, N = 4, 128, 512
FLOPS = 2 * 2 * G * D * D * N

F32 = mybir.dt.float32
BF16 = mybir.dt.bfloat16
U32 = mybir.dt.uint32
U8 = mybir.dt.uint8
FP8X4 = mybir.dt.float8_e4m3fn_x4
ACT = mybir.ActivationFunctionType
ALU = mybir.AluOpType

P = 128
PACK = 4
ROWS = D // PACK
HALVES = 2
C = N // HALVES
MM_N = 128
RUN = 4
SQUARE = 32
SCALAR_COLS_FIRST = 64
SCALAR_COLS = 96


def tile_rows_steps_tanh_kernel(tc, h, w1, x1, a1, w2, x2, out):
    nc = tc.nc

    with ExitStack() as ctx:
        sb = ctx.enter_context(tc.tile_pool(name="sb", bufs=1))
        ps = ctx.enter_context(tc.psum_pool(name="ps", bufs=1))
        ctx.enter_context(tc.manual_schedule())

        def tile(name, shape, dtype):
            return sb.tile(shape, dtype, name=name, align_bytes=64)

        def columns(half):
            return slice(half * C, (half + 1) * C)

        banks = [[ps.tile([P, N], F32, name="bank_%d_%d" % (half, g)) for g in range(G)] for half in range(HALVES)]

        def load_operand(name, src, cols):
            raw = tile(name, [P, PACK, cols.stop - cols.start], F32)
            nc.sync.dma_start(out=raw[:], in_=src.rearrange("g (p j) c -> (g p) j c", j=PACK)[:, :, cols])
            return raw[:]

        def load_addend(name, src, heads, cols):
            sbuf = tile(name, [P, len(heads), cols.stop - cols.start], F32)
            nc.sync.dma_start(out=sbuf[:], in_=src.rearrange("g m n -> m g n")[:, heads.start : heads.stop, cols])
            return [sbuf[:, g - heads.start, :] for g in heads]

        a_rows = tile("a_rows", [P, G * SQUARE], F32)
        nc.vector.memset(a_rows[:], 0.0)
        nc.scalar.dma_start(
            out=a_rows[0:P:SQUARE, :].rearrange("q (g i) -> q g i", g=G),
            in_=a1.rearrange("g (q i) o -> q g (i o)", i=SQUARE),
        )

        w1_raw = load_operand("w1_raw", w1, slice(0, D))
        h_raw = [load_operand("h_raw%d" % half, h, columns(half)) for half in range(HALVES)]
        x1_sb = [[] for half in range(HALVES)]
        for half in range(HALVES):
            for g0 in range(0, G, 2):
                x1_sb[half].extend(load_addend("x1_%d_%d" % (half, g0), x1, range(g0, g0 + 2), columns(half)))
        w2_raw = load_operand("w2_raw", w2, slice(0, D))

        x2_sb = load_addend("x2_0", x2, range(0, 1), slice(0, N))

        def interleave(name, raw, scalar_cols):
            width = raw.shape[2]
            grouped = tile(name, [P, width, PACK], BF16)
            split = width - scalar_cols
            for copy, lo, hi in ((nc.scalar.copy, split, width), (nc.vector.tensor_copy, 0, split)):
                if lo < hi:
                    copy(
                        out=grouped[:, lo:hi, :].rearrange("p (c i) j -> p c j i", i=RUN),
                        in_=raw[:, :, lo:hi].rearrange("p j (c i) -> p c j i", i=RUN),
                    )
            return grouped

        def quantize(name, grouped):
            width = grouped[:].shape[1]
            codes = tile(name + "_codes", [P, width], U32)
            scales = tile(name + "_scales", [P, width], U8)
            nc.vector.quantize_mx(
                out=codes[:].bitcast(FP8X4), scales=scales[:], in_=grouped[:].rearrange("p c j -> p (c j)")
            )
            return codes, scales

        def products(half, weights, state):
            (w_codes, w_scales), (s_codes, s_scales) = weights, state
            for g in range(G):
                rows = slice(g * ROWS, (g + 1) * ROWS)
                for c0 in range(0, C, MM_N):
                    cols = slice(c0, c0 + MM_N)
                    nc.tensor.matmul_mx(
                        out=banks[half][g][:, cols],
                        lhsT=w_codes[rows, :].bitcast(FP8X4),
                        lhsT_scale=w_scales[rows, :],
                        rhs=s_codes[rows, cols].bitcast(FP8X4),
                        rhs_scale=s_scales[rows, cols],
                        start=True,
                        stop=True,
                    )

        def add_tanh(name, half, g, addend):
            pre = tile(name + "_pre", [P, C], F32)
            nc.vector.tensor_tensor(out=pre[:], in0=banks[half][g][:, 0:C], in1=addend, op=ALU.add)
            act = tile(name + "_act", [P, C], F32)
            nc.scalar.activation(out=act[:], in_=pre[:], func=ACT.Tanh)
            return act

        a_cols = tile("a_cols", [P, G * SQUARE], F32)
        folded = [tile("folded%d" % half, [P, PACK, C], BF16) for half in range(HALVES)]
        tanh1 = {}

        def step1(half, g):
            tanh1[half, g] = add_tanh("step1_%d_%d" % (half, g), half, g, x1_sb[half][g])

        def scale_fold(half, g):
            h1 = tile("h1_%d_%d" % (half, g), [P, C], BF16)
            a_col = a_cols[:, SQUARE * g : SQUARE * g + 1]
            nc.vector.tensor_scalar(out=h1[:], in0=tanh1[half, g][:], scalar1=a_col, scalar2=None, op0=ALU.mult)
            nc.sync.dma_start(out=folded[half][g * ROWS : (g + 1) * ROWS, :, :], in_=h1[:])

        def step2(half, g):
            y = add_tanh("step2_%d_%d" % (half, g), half, g, x2_sb[g][:, columns(half)])
            nc.sync.dma_start(out=out[g, :, columns(half)], in_=y[:])

        w1_q = quantize("w1", interleave("w1_grouped", w1_raw, 0))
        products(0, w1_q, quantize("h_early", interleave("h_early_grouped", h_raw[0], SCALAR_COLS_FIRST)))
        h_late = interleave("h_late_grouped", h_raw[1], SCALAR_COLS)
        nc.vector.transpose(out=a_cols[:], in_=a_rows[:])
        step1(0, 0)
        products(1, w1_q, quantize("h_late", h_late))
        for g in range(1, G):
            step1(0, g)
        scale_fold(0, 0)
        scale_fold(0, 1)
        step1(1, 0)
        scale_fold(0, 2)
        scale_fold(0, 3)
        x2_sb.extend(load_addend("x2_1", x2, range(1, 2), slice(0, N)))
        for g in range(1, G):
            step1(1, g)
        for g in range(G):
            scale_fold(1, g)
        x2_sb.extend(load_addend("x2_2", x2, range(2, G), slice(0, N)))

        w2_grouped = interleave("w2_grouped", w2_raw, D)
        state0 = interleave("state0_grouped", folded[0][:], SCALAR_COLS)
        w2_q = quantize("w2", w2_grouped)
        products(0, w2_q, quantize("state0", state0))
        state1 = interleave("state1_grouped", folded[1][:], SCALAR_COLS)
        step2(0, 0)
        products(1, w2_q, quantize("state1", state1))
        for g in range(1, G):
            step2(0, g)
        for g in range(G):
            step2(1, g)
